import numpy as np, ml_dtypes
CORES = [5,29,101,125,133,157,229,253]
N = 8
BF = ml_dtypes.bfloat16
def gentries(a):
    return np.ascontiguousarray(a.reshape(8, 16, -1).transpose(0, 2, 1)).reshape(8, -1)
def gtable(e):
    e = np.asarray(e); return np.ascontiguousarray(e.reshape(8, -1, 16).transpose(0, 2, 1)).reshape(128, -1).astype(np.int32)
P, L, S, F, RO = 2048, 2048, 6, 256, 2
H = P - F
def depths(rng, up, top):
    s = np.where(rng.random((N, 8, P)) < up, 1, 1 - rng.geometric(0.5, (N, 8, P))); d = np.zeros((N, 8, P), np.int64); now = np.zeros((N, 8), np.int64)
    for v in range(1, P):
        now = np.minimum(np.maximum(now + s[:, :, v], 0), top); d[:, :, v] = now
    return d
def closed(d):
    e = np.zeros(d.shape, np.int64); last = np.full(d.shape[:-1] + (1,), P, np.int64)
    for k in range(int(np.max(d)) + 1):
        m = np.minimum.accumulate(np.where(d <= k, np.arange(P), P)[..., ::-1], axis=-1)[..., ::-1]
        e = np.where(d == k, np.concatenate([m[..., 1:], last], axis=-1), e)
    return e
def parts(rng):
    up = rng.choice(np.array([0.4, 0.5, 0.6]), (N, 8, 1)); top = rng.integers(3, 13, (N, 8))
    full = np.arange(P) < (P * rng.choice(np.array([8, 12, 14, 16]), (N, 8, 1))) // 16
    d = np.where(full, depths(rng, up, top), 0)
    x = np.where(rng.random((N, 8, 16, P)) < 0.25, rng.integers(0, 4, (N, 8, 16, P)), rng.integers(0, 256, (N, 8, 16, P))) * full[:, :, None, :]
    return x, d, rng.integers(0, 256, (N, 8, 16, L)), rng.integers(0, P, (N, 8, RO, L))
def pack(x, e, w, st):
    return {"x": np.ascontiguousarray(x.reshape(N, 128, P)).astype(np.float32).astype(BF), "w": np.ascontiguousarray(w.reshape(N, 128, L)).astype(np.float32).astype(BF),
            "ends": np.ascontiguousarray(e).astype(np.int32), "start": np.stack([gtable(a.reshape(8, -1)) for a in st])}
def setup_inputs(rng):
    x, d, w, st = parts(rng)
    return pack(x, closed(d), w, st)
def setup_inputs_room(rng):
    x, d, w, st = parts(rng); x = rng.integers(0, 256, x.shape); Q = P // 16; z = F // 4
    at = ((H - z, H), (H - z + 1, H + 1), (H, H + z), (H - 1, H - 1 + z), (P - z, P), (P - z + 1, P + 1), (P - 1, P - 1 + z), (H - z, -1))
    for q in range(N):
        for g in range(8):
            n = int(rng.integers(Q // 2, Q + 1)); a, b = at[(g + q) % 8]; a = a - n; b = P if b < 0 else b - n; D = d[q, g].copy()
            d[q, g] = np.concatenate([np.tile(np.arange(3), Q), D[:a - 3 * Q], np.zeros(1, np.int64), 1 + D[:b - a - 1], D[:P - b]])
            hot = 3 * rng.permutation(Q)[:n]
            st[q, g, 0] = rng.permutation(np.concatenate([hot, rng.choice(hot, L - n)]))
    return pack(x, closed(d), w, st)
def setup_inputs_ties(rng):
    x, d, w, st = parts(rng); lo = rng.choice(np.array([0, 100, 252]), (N, 8, 1, 1))
    x = lo + rng.integers(0, 4, x.shape); x[:, 1::2] = (lo + 2 * rng.integers(0, 2, (N, 8, 1, P)))[:, 1::2]
    return pack(x, closed(d), np.minimum(lo + rng.integers(0, 5, w.shape), 255), st)
def setup_inputs_alike(rng):
    x, d, w, st = parts(rng); x = rng.integers(0, 256, x.shape); e = closed(d); at = np.arange(P)
    names = rng.integers(0, P, (N, 8, RO, 6)); names[..., 0] = 0; names[..., 1] = P - 1
    st = np.take_along_axis(names, rng.integers(0, 6, st.shape), 3)
    for q in range(N):
        g = (np.arange(4) + q) % 8
        e[q, g[0]] = P; st[q, g[0], 0] = rng.choice(np.array([0, P - 1, P - 2, P - 3, P - 1 - S, P - 2 - S]), L)
        e[q, g[1]] = at + 1; e[q, g[1], :2] = P; st[q, g[1], 0] = 0
        e[q, g[2]] = at + 1
        e[q, g[3]] = np.where(at % 2 == 0, P, at + 1); st[q, g[3], 0] = rng.integers(0, P, L)
    return pack(x, e, w, st)
def setup_inputs_far(rng):
    x, d, w, st = parts(rng); x = rng.integers(0, 256, x.shape); w = rng.integers(1, 256, w.shape); g = rng.permutation(8); odd = np.arange(N) % 2 == 1; i4 = np.arange(16)[:, None] % 4
    kid = np.where(odd, rng.integers(3 * P // 4 + 2, P - 1, N), P - 1); low = np.where(odd, rng.integers(3 * P // 4, H, N), P - 1)
    left = np.where(odd, rng.integers(15 * P // 32, P // 2 - 4, N), rng.integers(7 * P // 16 + 1, 15 * P // 32, N)); T = min(P // 7, L // 4)
    st[:, g[:4]] = P - 1
    for q in range(N):
        D = d[q].copy(); b = int(kid[q]); z = int(low[q]); s = int(left[q]); m = D[g[0]]
        d[q, g[0]] = np.concatenate([np.array([0, 1, 2, 3]), 3 + m[:b - 4], np.array([2]), m[:P - b - 1]])
        x[q, g[0], :, b] = 0; st[q, g[0], 0] = 0
        d[q, g[1]] = np.concatenate([np.zeros(z + 1, np.int64), D[g[1]][:P - z - 1]])
        v = rng.choice(np.array([0, z - 2]), L); v[0] = 0; v[1] = z - 2; st[q, g[1], 0] = v
        m = D[g[2]]; d[q, g[2]] = np.concatenate([np.arange(3), 2 + m[:s - 1], m[:P - s - 2]]); st[q, g[2], 0] = 0
        m = D[g[3]]; a = H - 4 + q % 2
        d[q, g[3]] = np.concatenate([m[:H - 4], np.array([0, 0, 1, 2, 3]) if q % 2 else np.array([0, 1, 2, 3, 3]), m[:P - H - 1]])
        v = np.where(rng.random(L) < 0.5, a, rng.integers(H, P, L)); v[0] = a; st[q, g[3], 1] = v
        d[q, g[4]] = np.concatenate([np.tile(np.array([0, 1, 2, 2, 1, 2, 2]), T), D[g[4]][:P - 7 * T]])
        few = np.array([4, 0, 2, 3, 1, 2, 3])[np.arange(P) % 7]
        x[q, g[4]] = np.where(i4 == few, rng.integers(0, 61, (16, P)), rng.integers(200, 256, (16, P)))
        j = rng.permutation(np.concatenate([np.arange(4 * T), rng.integers(0, 4 * T, L - 4 * T)])); st[q, g[4], 0] = 7 * (j // 4)
        w[q, g[4]] = np.where((i4 == (j % 4) // 2) | (i4 == 2 + j % 2), rng.integers(100, 201, (16, L)), 0)
    x[:, g[0], :, 2] = 255; x[:, g[0], :, 3] = 0; x[:, g[0], :, 4] = 255; x[:, g[3], :, H - 1] = 255; x[:, g[3], :, H] = 0
    for k in (1, 2):
        x[:, g[k], :, 2] = 0; x[:, g[k], :, 3] = 255
    e = closed(d)
    for q in range(N):
        z = int(low[q]); e[q, g[1], :z + 1] = z + 1; e[q, g[1], 2] = 3
    return pack(x, e, w, st)
def setup_inputs_spread(rng):
    x, d, w, st = parts(rng)
    d = depths(rng, 0.35 + 0.35 * rng.random((N, 8, 1)), np.exp2(1 + 5 * rng.random((N, 8))).astype(np.int64) + 1)
    x = np.minimum((np.exp2(8 * rng.random((N, 8, 1, P))) * rng.random((N, 8, 16, P))).astype(np.int64), 255)
    w = np.minimum((np.exp2(8 * rng.random((N, 8, 1, L))) * rng.random((N, 8, 16, L))).astype(np.int64), 255)
    st = np.minimum((P * rng.random((N, 8, RO, L)) ** rng.choice(np.array([1, 2, 4]), (N, 8, 1, 1))).astype(np.int64), P - 1)
    return pack(x, closed(d), w, st)
def check_inputs(d):
    bad = []
    for k in ("x", "w"):
        v = d[k].astype(np.float32)
        if not np.all((v >= 0) & (v <= 255) & (v == np.floor(v))): bad.append("whole numbers from 0 to 255 in " + k)
    e = d["ends"].astype(np.int64); n = e - np.arange(P)
    if np.min(n) < 1 or np.max(e) > P: bad.append("range of ends")
    else:
        big = e; most = np.zeros(e.shape, np.int64); k = 1
        while k <= P:
            sel = (n >= k) & (n < 2 * k)
            most = np.where(sel, np.maximum(big, np.take_along_axis(big, np.where(sel, e - k, 0), 2)), most)
            big = np.concatenate([np.maximum(big[..., :P - k], big[..., k:]), big[..., P - k:]], axis=2); k = 2 * k
        if np.any(most > e): bad.append("runs that cross")
    if np.min(d["start"]) < 0 or np.max(d["start"]) > P - 1: bad.append("range of start")
    return bad
def grow(x, e, w, v):
    G = np.arange(8)[:, None]; at = np.arange(P); n = np.zeros((8, L), np.int64); par = v
    for i in range(S):
        ev = e[G, v]; a = np.minimum(v + 1, P - 1); b = e[G, a]; kids = ev > v + 1; two = kids & (b < ev); b = np.minimum(b, P - 1)
        ra = np.add.reduce(np.maximum(w - x[G, a], 0), axis=2); rb = np.add.reduce(np.maximum(w - x[G, b], 0), axis=2)
        par = np.where(kids, v, par); n = n + kids; v = np.where(kids, np.where(two & (rb > ra), b, a), v)
    hit = (n >= 2) & (e[G, v] == v + 1); gi = np.broadcast_to(G, v.shape)[hit]
    head = np.zeros((8, P), bool); head[gi, v[hit]] = True; mark = np.zeros((8, P), bool); mark[gi, par[hit]] = True
    zero = np.zeros((8, 1), np.int64); reach = np.maximum.accumulate(np.where(mark, e, 0), axis=1)
    top = mark & (np.concatenate([zero, reach[:, :-1]], axis=1) <= at); inside = reach > at; keep = ~head
    first = np.maximum.accumulate(np.where(top, at, 0), axis=1)
    K = np.concatenate([zero, np.add.accumulate(keep.astype(np.int64), axis=1)], axis=1)
    M = np.concatenate([zero, np.add.accumulate(keep * (1 + 2 * inside), axis=1)], axis=1)
    size = np.where(inside, K[G, e] - K[:, :P], M[G, e] - M[:, :P]); s = K[G, e[G, first]] - K[G, first]
    nx = np.zeros((8, P, 16), np.int64); ne = np.zeros((8, P), np.int64) + at + 1
    for c in range(3):
        q = np.where(inside, M[G, first] + c * s + K[:, :P] - K[G, first], M[:, :P])
        gk, vk = np.nonzero(keep & (inside | (c == 0)) & (q < P)); qk = q[gk, vk]
        nx[gk, qk] = np.maximum(x[gk, vk] - c, 0); ne[gk, qk] = qk + size[gk, vk]
    return nx, ne
def reference(x, w, ends, start):
    X = np.ascontiguousarray(x.astype(np.float32).astype(np.int64).reshape(N, 8, 16, P).transpose(0, 1, 3, 2)); E = ends.astype(np.int64)
    W = np.ascontiguousarray(w.astype(np.float32).astype(np.int64).reshape(N, 8, 16, L).transpose(0, 1, 3, 2))
    st = np.stack([gentries(a) for a in start]).astype(np.int64).reshape(N, 8, RO, L)
    for t in range(RO):
        both = [grow(X[r], E[r], W[r], st[r, :, t]) for r in range(N)]
        gx = np.stack([a for a, b in both]); ge = np.stack([b for a, b in both])
        X = np.concatenate([gx[:, :, :H], np.roll(gx[:, :, H:], 1, axis=0)], axis=2)
        E = np.concatenate([np.minimum(ge[:, :, :H], H), np.roll(np.minimum(ge[:, :, H:], P), 1, axis=0)], axis=2)
    return {"y": np.ascontiguousarray(X.transpose(0, 1, 3, 2)).reshape(N, 128, P).astype(np.float32).astype(BF), "ye": E.astype(np.float32)}

from concourse.mybir import dt, AluOpType, AxisListType, ActivationFunctionType

A = AluOpType
AF = ActivationFunctionType
P = 2048
SC = 12
VC = 64 - SC
NVR = 40
XW = 2064
CUT = 1792
SWW = 8192

BLK = ["VF", "V1", "Q2", "ZERO", "two", "nhE", "hv", "KX", "HS", "HI", "mE", "ks", "kx", "K2", "FM", "Fs", "ex", "nex", "eq", "en",
       "PF", "NB", "NN", "PN", "SP", "cc", "s", "L3", "tA", "tC", "tD", "EN", "HIw", "LOw", "NLO", "VAL", "nv", "hiF", "qq", "csb",
       "ID", "TRI", "SHIFT", "SHR", "SHL", "RST", "MK0", "ONEF", "rowA", "rowB", "rowC", "rowD", "rowN", "rowT"]
SCRATCH = {"BK": ("sbuf", [128, 128 * len(BLK)], "float32")}
for n_ in ("E0", "E1", "E2", "hm", "RCH", "RC2", "CSs"):
    SCRATCH[n_] = ("sbuf", [128, 132], "float32")
for n_ in ("VI", "vint", "hii", "loi"):
    SCRATCH[n_] = ("sbuf", [128, 128], "int32")
for n_ in ("B16", "EL16", "off16", "q16", "L316", "LS16", "Z16", "SBE", "RLE0", "RLE1", "LE0", "LE1"):
    SCRATCH[n_] = ("sbuf", [128, 128], "uint16")
for n_ in ("IH", "IDB", "NIDB", "hmb", "kb", "kl", "bb", "bl", "sb", "sl", "nb", "nl"):
    SCRATCH[n_] = ("sbuf", [128, 128], "bfloat16")
for n_ in ("F1", "FP", "FN", "FA", "FB", "ONEB", "LOI"):
    SCRATCH[n_] = ("sbuf", [128, 144], "bfloat16")
for n_ in ("XPHI", "GR", "GK", "W", "KT", "ST", "HMR", "VD", "Y2", "R0", "R1"):
    SCRATCH[n_] = ("sbuf", [128, 2048], "bfloat16")
SCRATCH.update({
    "X0": ("sbuf", [128, 3 * XW], "bfloat16"), "X1": ("sbuf", [128, 3 * XW], "bfloat16"),
    "XBS": ("sbuf", [128, XW], "bfloat16"), "MB": ("sbuf", [128, XW], "bfloat16"),
    "SW": ("sbuf", [128, SWW], "bfloat16"),
    "LH": ("sbuf", [128, 128 * 128], "bfloat16"), "RH": ("sbuf", [128, 128 * 130], "bfloat16"),
    "ST0": ("sbuf", [128, 256], "int32"), "EI": ("sbuf", [128, 128], "int32"),
    "cols": ("sbuf", [128, 32], "float32"), "coli": ("sbuf", [128, 8], "int32"),
    "SBX": ("sbuf", [128, 256], "bfloat16"), "RLX0": ("sbuf", [128, 256], "bfloat16"), "RLX1": ("sbuf", [128, 256], "bfloat16"),
})
for n_ in (0, 1):
    SCRATCH["MR%d" % n_] = ("sbuf", [128, 1024], "bfloat16")
    SCRATCH["WD%d" % n_] = ("sbuf", [128, 32 * SC], "bfloat16")
    SCRATCH["GS%d" % n_] = ("sbuf", [128, 32 * SC], "bfloat16")
    SCRATCH["ZF%d" % n_] = ("sbuf", [128, 128], "float32")
for n_ in range(8):
    SCRATCH["p%d" % n_] = ("psum", [128, 512], "float32")
SEMAPHORES = ["q_v", "q_s", "q_t", "q_g"] + ["d%d" % k for k in range(40)] + \
    [a + b for a in ("rx", "rn", "lx", "le", "ax", "ae") for b in "01"]
NX, NE = 8, 4


def pick(topo, src, dst, k, skip=0):
    return sum(1 << e for e in topo.engines(src, dst)[skip:skip + k])


def relays(topo, core, dst):
    return [c for c in topo.cores_of(core) if c != core and topo.die(c) == topo.die(core) and topo.may_write(c, dst)]


def relay_program(g, core, T, topo):
    for r, me in enumerate(T.cores):
        dst = T.cores[(r + 1) % len(T.cores)]
        rl = relays(topo, me, dst)
        if core not in rl[:2]:
            continue
        rid, pid = topo.addr(dst, core)
        if core == rl[0]:
            for t in range(2):
                g.wait_ge(T.sem["rx%d" % t], NX)
                out = T.X1[:, CUT:P] if t == 0 else T.Y2[:, CUT:P]
                g.remote_dma(out, T["RLX%d" % t][:], T.sem["ax%d" % t], T.sem["lx%d" % t], pid, rid, pick(topo, core, dst, NX))
            for t in range(2):
                g.wait_ge(T.sem["lx%d" % t], NX)
        else:
            for t in range(2):
                g.wait_ge(T.sem["rn%d" % t], NE)
                g.remote_dma(T["LE%d" % t][:], T["RLE%d" % t][:], T.sem["ae%d" % t], T.sem["le%d" % t], pid, rid, pick(topo, core, dst, NE))
            for t in range(2):
                g.wait_ge(T.sem["le%d" % t], NE)


def rank_program(g, core, T, topo):
    if T.rank_of(core) is None:
        return relay_program(g, core, T, topo)
    rank = T.rank_of(core)
    dst = T.cores[(rank + 1) % len(T.cores)]
    rl = relays(topo, core, dst)
    queues = {"v": g.vector, "s": g.scalar, "t": g.tensor, "g": g, "y": g.sync}
    count = {}
    known = {q: {} for q in queues}
    log = {}
    nd = [0]
    where = {n: 128 * k for k, n in enumerate(BLK)}

    def r(name, lo=0, hi=None, step=None, p=None, tag=None):
        if name in where:
            hi = 128 if hi is None else hi
            lo, hi, name = lo + where[name], hi + where[name], "BK"
        t = T[name]
        hi = t.shape[1] if hi is None else hi
        pp = slice(None) if p is None else p
        return (t[pp, lo:hi] if step is None else t[pp, lo:hi:step], name, lo, hi, tag)

    def rev(name, p=None):
        o = where[name]
        return (T.BK[slice(None) if p is None else p, o + 127:(o - 1 if o else None):-1], "BK", o, o + 128, None)

    def ind(name, lo, hi, lname, a, b):
        return (T[name][:, lo:hi].indirect(T[lname][:, a:b]), name, lo, hi, None, (None, lname, a, b, None))

    def need(q, reads, writes):
        want = {}
        for is_w, views in ((False, reads), (True, writes)):
            for v in views:
                bank = v[1][0] == "p" and v[1][1:].isdigit()
                for e in log.get(v[1], ()):
                    same = e[4] == q
                    if same and q == "t":
                        continue
                    if (same or not bank) and (e[0] >= v[3] or v[2] >= e[1] or (e[2] is not None and v[4] is not None and e[2] != v[4])):
                        continue
                    if not is_w and not e[3] and (same or not bank):
                        continue
                    old = want.get(e[5])
                    if old is None or old[0] < e[6]:
                        want[e[5]] = (e[6], e[7])
        kn = known[q]
        for sem in sorted(want, key=lambda k: -len(want[k][1])):
            val, clock = want[sem]
            if kn.get(sem, 0) >= val:
                continue
            queues[q].wait_ge(T.sem[sem], val)
            for k2, v2 in clock.items():
                if kn.get(k2, 0) < v2:
                    kn[k2] = v2
            kn[sem] = val

    def note(q, reads, writes, sem, val, clock):
        for is_w, views in ((False, reads), (True, writes)):
            for v in views:
                L = log.setdefault(v[1], [])
                if is_w:
                    L[:] = [e for e in L if not (v[2] <= e[0] and e[1] <= v[3] and (v[4] is None or v[4] == e[2]))]
                else:
                    L[:] = [e for e in L if not (not e[3] and e[4] == q and q != "dma" and e[0] >= v[2] and e[1] <= v[3])]
                L.append([v[2], v[3], v[4], is_w, q, sem, val, clock])

    def op(q, reads, writes, calls):
        reads = list(reads) + [v[5] for v in list(reads) + list(writes) if len(v) > 5]
        need(q, reads, writes)
        sem = "q_" + q
        for call in calls:
            call().then_inc(T.sem[sem], 1)
            count[sem] = count.get(sem, 0) + 1
        clock = dict(known[q])
        clock[sem] = count[sem]
        note(q, reads, writes, sem, count[sem], clock)

    def dma(q, out, in_, ext_in=False):
        sem = "d%d" % nd[0]
        nd[0] += 1
        reads, writes = ([] if ext_in else [in_]), ([out])
        need(q, reads, writes)
        queues[q].dma_start(out[0], in_[0]).then_inc(T.sem[sem], 16)
        count[sem] = 16
        clock = dict(known[q])
        clock[sem] = 16
        note("dma", reads, writes, sem, 16, clock)

    def ext(ap, name, lo=0, hi=2048):
        return (ap, "#" + name, lo, hi, None)

    def rows(name, k, lo, n, src):
        dma("y", (T[name][k:128:16, lo:lo + n], name, lo, lo + n, "row%d" % k), src)

    V, S, TE = g.vector, g.scalar, g.tensor

    def tt(out, a, b, o):
        op("v", [a, b], [out], [lambda: V.tensor_tensor(out[0], a[0], b[0], o)])

    def ts(out, a, s1, s2, o0, o1=None):
        rd = [a] + [s for s in (s1, s2) if isinstance(s, tuple)]
        x1 = s1[0] if isinstance(s1, tuple) else s1
        x2 = s2[0] if isinstance(s2, tuple) else s2
        if o1 is None:
            op("v", rd, [out], [lambda: V.tensor_scalar(out[0], a[0], x1, None, o0)])
        else:
            op("v", rd, [out], [lambda: V.tensor_scalar(out[0], a[0], x1, x2, o0, o1)])

    def tc(out, a):
        op("v", [a], [out], [lambda: V.tensor_copy(out[0], a[0])])

    def fill(out, val):
        op("v", [], [out], [lambda: V.memset(out[0], val)])

    def scan(out, d0, d1, o0, o1):
        op("v", [d0, d1], [out], [lambda: V.tensor_tensor_scan(out[0], d0[0], d1[0], 0.0, o0, o1)])

    def act(out, a, f, bias=0.0):
        rd = [a] + ([bias] if isinstance(bias, tuple) else [])
        bb = bias[0] if isinstance(bias, tuple) else bias
        op("s", rd, [out], [lambda: S.activation(out[0], a[0], f, bias=bb, scale=1.0)])

    def mm(bank, c0, c1, lhs, rhs, p=None):
        out = r(bank, c0, c1, p=p)
        op("t", [lhs, rhs], [out], [lambda: TE.matmul(out[0], lhs[0], rhs[0], True, True)])

    def conv(bank, c0, parts):
        n = parts[0][4]
        out = r(bank, c0, c0 + n)
        for k, (F, name, base, nat, nn) in enumerate(parts):
            calls = []
            for i in range(16):
                lhs = T[F][:, 15 - i:143 - i]
                rhs = T[name][:, base + 128 * i:base + 128 * i + nn] if nat else T[name][:, base + i:base + 16 * nn:16]
                st, sp = (k == 0 and i == 0), (k == len(parts) - 1 and i == 15)
                calls.append(lambda lhs=lhs, rhs=rhs, st=st, sp=sp: TE.matmul(out[0], lhs, rhs, st, sp))
            rv = r(name, base, base + (2048 if nat else 16 * nn))
            op("t", [r(F), rv], [out], calls)

    def col(k):
        return r("cols", k, k + 1)

    def slot(k):
        return r("p7", 128 * k, 128 * k + 128)

    pVF, pV1, pQN, pVB = [r("p6", 128 * k, 128 * k + 128) for k in range(4)]
    p1 = slice(0, 1)

    dma("y", r("EI"), ext(T.ends[:], "ends"), True)
    dma("s", r("X0", 0, P), ext(T.x[:], "x"), True)
    dma("y", r("ST0"), ext(T.start[:], "start"), True)
    dma("y", r("W"), ext(T.w[:], "w"), True)
    for h in range(2):
        for k in range(2):
            dma("y", r("WD%d" % h, 16 * SC * k, 16 * SC * (k + 1)), ext(T.w[:, 1024 * h + 16 * VC:1024 * h + 1024], "w"), True)

    def iota(out, pat, base, cm, small=True):
        op("g", [], [out], [lambda: g.iota(out[0], pat, base, cm, allow_small_or_imprecise_dtypes=True) if small else g.iota(out[0], pat, base, cm)])

    def asel(out, in_, pat, cmp, fl, base, cm):
        op("g", [in_], [out], [lambda: g.affine_select(out[0], in_[0], pat, cmp, fl, base, cm)])

    fill(r("ONEF"), 1.0)
    fill(r("ONEB"), 1.0)
    fill(r("MB"), 0.0)
    fill(r("XBS", 0, 16), 0.0)
    fill(r("XBS", P, XW), 0.0)
    fill(r("X0", P, XW), 0.0)
    fill(r("X1", P, XW), 0.0)
    fill(r("ZERO"), 0.0)
    iota(r("VI"), [[1, 128]], 0, 128, False)
    asel(r("SHIFT"), r("ONEF"), [[-1, 128]], A.is_equal, 0.0, -1, 1)
    asel(r("SHIFT"), r("SHIFT"), [[0, 8], [1, 16]], A.not_equal, 0.0, -15, 0)
    iota(r("coli", 0, 1), [[0, 1]], 0, 1, False)
    asel(r("F1"), r("ONEB"), [[-16, 9], [0, 16]], A.is_ge, 0.0, 0, 1)
    asel(r("F1"), r("F1"), [[16, 9], [0, 16]], A.is_ge, 0.0, 15, -1)
    asel(r("F1"), r("F1"), [[0, 9], [1, 16]], A.is_equal, 0.0, -15, 0)
    asel(r("IDB"), r("ONEB", 0, 128), [[-1, 128]], A.is_equal, 0.0, 0, 1)
    iota(r("IH"), [[0, 8], [1, 16]], 1, 0)
    asel(r("IH"), r("IH"), [[-16, 8], [0, 16]], A.is_ge, -1000.0, 0, 1)
    asel(r("IH"), r("IH"), [[16, 8], [0, 16]], A.is_ge, -1000.0, 15, -1)
    iota(r("LOI", 0, 130), [[1, 130]], -1, 0)
    asel(r("TRI"), r("ONEF"), [[-16, 8], [0, 16]], A.is_ge, 0.0, 0, 1)
    asel(r("TRI"), r("TRI"), [[16, 8], [0, 16]], A.is_ge, 0.0, 15, -1)
    asel(r("TRI"), r("TRI"), [[1, 128]], A.is_ge, 0.0, -1, -1)
    asel(r("RST"), r("ONEF"), [[0, 8], [1, 16]], A.not_equal, 0.0, 0, 0)
    asel(r("MK0"), r("ONEF"), [[0, 8], [1, 16]], A.is_equal, 0.0, 0, 0)
    asel(r("SHR"), r("RST"), [[-1, 128]], A.is_equal, 0.0, 1, 1)
    asel(r("SHL"), r("RST"), [[1, 128]], A.is_equal, 0.0, -128, 1)
    asel(r("ID"), r("ONEF"), [[-1, 128]], A.is_equal, 0.0, 0, 1)
    iota(r("LH", 0, 2048), [[0, 128], [128, 16]], 0, 0)
    iota(r("LH", 2048, 4096), [[1, 128], [0, 16]], 1, 0)
    ts(r("VI"), r("VI"), 2047, None, A.bitwise_and)
    tc(r("VF"), r("VI"))
    tc(pVF, r("VI"))
    ts(r("V1"), r("VF"), 1.0, None, A.add)
    ts(pV1, r("VF"), 1.0, None, A.add)

    def later():
        for n in ("HMR", "KT", "ST", "VD"):
            iota(r(n), [[0, 2048]], 0, 0)
        dma("y", (T.VD[0:128:16, :], "VD", 0, 2048, "a"), r("LH", 0, 2048, p=slice(0, 128, 16)))
        dma("y", (T.VD[1:128:16, :], "VD", 0, 2048, "b"), r("LH", 2048, 4096, p=slice(1, 128, 16)))
        ts(pVB, r("VF"), 6145.0, None, A.add)
        ts(pQN, r("VF"), -1.0, 8192.0, A.mult, A.add)
        ts(r("Q2"), r("VF"), 2.0, -8192.0, A.mult, A.add)
        ts(r("coli", 1, 2), r("coli", 0, 1), 15, None, A.bitwise_and)
        tc(col(0), r("coli", 1, 2))
        ts(col(1), col(0), 2.0, None, A.is_lt)
        ts(col(2), col(0), 14.0, None, A.is_lt)
        ts(col(3), col(0), 14.0, None, A.is_ge)
        ts(col(4), col(3), 256.0, 1792.0, A.mult, A.add)
        ts(r("FA"), r("F1"), col(1), None, A.mult)
        tt(r("FB"), r("F1"), r("FA"), A.subtract)

    def table_start(t):
        E = "E%d" % t
        mm("p0", 0, 1, r("SHIFT"), r(E, 0, 1))
        tt(slot(0), r(E, 0, 128), pV1, A.is_gt)
        tt(slot(1), r("VF"), slot(0), A.add)
        tc(r(E, 128, 129), r("p0", 0, 1))
        tt(slot(2), r(E, 1, 129), r(E, 0, 128), A.is_lt)
        tt(r("tC"), slot(2), r(E, 1, 129), A.mult)
        tt(slot(2), slot(1), r("tC"), A.max)
        tc(r("B16"), slot(2))
        tc(r("bb"), slot(2))
        tt(r("bl"), slot(2), r("bb"), A.subtract)
        rows("MB", 0, 1, P, r("bb"))
        rows("MB", 1, 1, P, r("bl"))
        tt(r("nhE"), slot(0), r(E, 0, 128), A.mult)
        ts(slot(3), slot(0), 1.0e6, None, A.mult)
        ts(r("EL16"), r(E, 0, 128), -1.0, None, A.add)
        for h in range(2):
            a = 128 * t + 64 * h
            ts(r("Z16", 64 * h, 64 * h + 64), r("ST0", a, a + 64), 1.0, None, A.add)
            ts(r("ZF%d" % h, 0, 64), r("ST0", a, a + 64), 1.0, None, A.add)

    def permute(eng, dst_, off, src, blocks, base=0):
        for i in blocks:
            o = r(dst_, off + 128 * (i - base), off + 128 * (i - base) + 128)
            a = r(src, i, 2048, 16)
            if eng == "v":
                tc(o, a)
            else:
                act(o, a, AF.Copy)

    tc(r("E0", 0, 128), r("EI"))
    table_start(0)
    ts(r("FP"), r("F1"), 4096.0, None, A.mult)
    ts(r("FN"), r("F1"), -4096.0, None, A.mult)
    ts(r("NIDB"), r("IDB"), -1.0, None, A.mult)
    later()

    def j_gather(h, which, t):
        win, base = ("X%d" % t, 0) if which == 0 else ("XBS", 1024)
        tt(r("R%d" % h, base, base + 16 * VC), ind(win, 0, XW, "Z16", 64 * h, 64 * h + VC), r("W", 1024 * h, 1024 * h + 16 * VC), A.min)

    def s_gather(h, t):
        n = 16 * SC
        for k, win in enumerate(("XBS", "X%d" % t)):
            act(r("GS%d" % h, n * k, n * k + n), ind(win, 0, XW, "Z16", 64 * h + VC, 64 * h + 64), AF.Copy)
        o = r("p%d" % (4 + h), 0, 2 * n)
        op("t", [r("IDB"), r("NIDB"), r("WD%d" % h), r("GS%d" % h)], [o],
           [lambda: TE.matmul(o[0], T.IDB[:], T["WD%d" % h][:], True, False),
            lambda: TE.matmul(o[0], T.NIDB[:], T["GS%d" % h][:], False, True)])

    def s_meta(h):
        act(r("MR%d" % h), ind("MB", 0, XW, "Z16", 64 * h, 64 * h + 64), AF.Copy)
        conv("p%d" % (2 + h), 0, [("F1", "MR%d" % h, 0, False, 64)])

    def s_relu(h):
        n = 16 * SC
        for k in range(2):
            act(r("R%d" % h, 1024 * k + 16 * VC, 1024 * k + 1024), r("p%d" % (4 + h), n * k, n * k + n), AF.Relu)
        conv("p%d" % h, 0, [("FP", "R%d" % h, 0, False, 64), ("FN", "R%d" % h, 1024, False, 64)])

    def decide(h, step):
        z0 = 64 * (step % 2)
        z1 = 64 - z0
        zf = "ZF%d" % h
        a, b = 64 * h, 64 * h + 64
        nv = r("nv", a, b)
        tt(r("tA", a, b), r("p%d" % h, 0, 64), r(zf, z0, z0 + 64), A.max)
        tt(nv, r("p%d" % (2 + h), 0, 64), r("tA", a, b), A.min)
        if step < 5:
            ts(r("Z16", a, b), nv, 1.0, None, A.add)
            ts(r(zf, z1, z1 + 64), nv, 1.0, None, A.add)
        if step == 1:
            tt(r("VAL", a, b), r(zf, z1, z1 + 64), r(zf, z0, z0 + 64), A.not_equal)
        if step == 5:
            tc(r("vint", a, b), nv)
            ts(r("hii", a, b), r("vint", a, b), 7, None, A.arith_shift_right)
            ts(r("loi", a, b), r("vint", a, b), 127, None, A.bitwise_and)
            ts(r("hiF", a, b), r("hii", a, b), 1.0, None, A.add)
            ts(r("NLO", a, b), r("loi", a, b), -1.0, 0.5, A.mult, A.add)
            tc(r("LOw", a, b), r("loi", a, b))
            tt(r("HIw", a, b), r("hiF", a, b), r("VAL", a, b), A.mult)

    def walks(t):
        g2(None, "X%d" % t, XW, "B16", None, "XPHI")
        permute("s", "XBS", 1, "XPHI", range(6))
        permute("v", "XBS", 1, "XPHI", range(6, 16))
        for s in range(12):
            h = s % 2
            s_gather(h, t)
            s_meta(h)
            j_gather(h, 0, t)
            j_gather(h, 1, t)
            s_relu(h)
            if s:
                decide(1 - h, (s - 1) // 2)
        decide(1, 5)

    def hist():
        order = []
        kv = 0
        for c in range(128):
            want = (NVR * (c + 1)) // 128
            order.append(("V" if want > kv else "S", c))
            kv = max(kv, want)
        vs = [c for e, c in order if e == "V"]
        ss = [c for e, c in order if e == "S"]
        for e, c in order:
            lh = r("LH", 128 * c, 128 * c + 128)
            ts(lh, r("IH"), r("HIw", c, c + 1), None, A.is_equal)
            if e == "V":
                rh = r("RH", 130 * c, 130 * c + 128)
                ts(rh, r("LOI", 1, 129), r("LOw", c, c + 1), None, A.is_equal)
                bank, n, st, sp = "p4", 128, c == vs[0], c == vs[-1]
            else:
                rh = r("RH", 130 * c, 130 * c + 129)
                act(rh, r("LOI", 0, 129), AF.Sign, r("NLO", c, c + 1))
                bank, n, st, sp = "p5", 129, c == ss[0], c == ss[-1]
            o = r(bank, 0, n)
            op("t", [lh, rh], [o], [lambda: TE.matmul(o[0], lh[0], rh[0], st, sp)])

    def g2(bank, src, W, lname, F, out):
        o, i = r(out, 0, 1024), ind(src, 0, W, lname, 0, 64)
        op("v", [i], [o], [lambda: V.tensor_copy(o[0], i[0])])
        act(r(out, 1024, 2048), ind(src, 0, W, lname, 64, 128), AF.Copy)
        if F is not None:
            for k in range(2):
                conv(bank, 64 * k, [(F, out, 1024 * k, False, 64)])

    def row(name):
        return r(name, p=p1)

    def grow(t):
        X = "X%d" % t
        XN, EX = ("X1" if t == 0 else "Y2"), "E%d" % (t + 1)
        HM = r("hm", 0, 128)
        act(r("CSs", 0, 129), r("p5", 0, 129), AF.Copy)
        act(r(X, XW, XW + P), r(X, 0, P), AF.Relu, -1.0)
        tt(r("tA"), r("p5", 1, 129), r("CSs", 0, 128), A.subtract)
        tt(slot(0), r("p4", 0, 128), r("tA"), A.add)
        tc(r("tC"), slot(3))
        tt(HM, slot(0), r("tC"), A.is_gt)
        tc(r("hmb"), HM)
        rows("HMR", 0, 0, P, r("hmb"))
        mm("p0", 0, 1, r("SHIFT"), r("hm", 0, 1))
        scan(r("HS"), HM, r("ZERO"), A.add, A.add)
        mm("p1", 0, 1, r("TRI"), r("HS", 127, 128))
        tc(r("hm", 128, 129), r("p0", 0, 1))
        tt(r("hv"), HM, pVB, A.mult)
        ts(r("HI"), r("HS"), r("p1", 0, 1), None, A.add)
        tt(slot(1), r("HI"), pV1, A.subtract)
        tt(r("KX"), HM, slot(1), A.subtract)
        ts(r("kb"), slot(1), -1.0, None, A.mult)
        tt(r("tA"), slot(1), r("kb"), A.add)
        ts(r("kl"), r("tA"), -1.0, None, A.mult)
        ts(col(12), r("KX", 127, 128), r("hm", 127, 128), None, A.subtract)
        rows("KT", 0, 0, P, r("kb"))
        rows("KT", 1, 0, P, r("kl"))
        fill(r("SW", 0, 2048), 0.0)
        g2("p2", "HMR", P, "B16", "F1", "GR")
        tt(slot(0), r("p2", 0, 128), r("hm", 1, 129), A.max)
        tt(r("mE"), slot(0), r("nhE"), A.mult)
        scan(r("RCH", 1, 129), r("mE"), r("ZERO"), A.max, A.add)
        mm("p3", 0, 128, r("RCH", 128, 129), r("SHR"), p=p1)
        scan(row("rowA"), row("RST"), r("p3", 0, 128, p=p1), A.mult, A.max)
        mm("p3", 200, 201, row("rowA"), r("ONEF", 0, 1, p=p1))
        ts(r("RC2", 1, 129), r("RCH", 1, 129), r("p3", 200, 201), None, A.max)
        tc(r("RC2", 0, 1), r("p3", 200, 201))
        tt(slot(3), r("RC2", 1, 129), pVF, A.is_gt)
        tt(slot(1), slot(3), HM, A.subtract)
        scan(r("ks"), slot(1), r("ZERO"), A.add, A.add)
        mm("p4", 0, 1, r("TRI"), r("ks", 127, 128))
        tt(r("kx"), slot(1), r("ks"), A.subtract)
        tt(slot(2), r("RC2", 0, 128), pVF, A.is_le)
        ts(r("K2"), r("kx"), r("p4", 0, 1), -2.0, A.subtract, A.mult)
        tt(r("FM"), slot(2), r("K2"), A.mult)
        scan(r("Fs"), r("FM"), r("ZERO"), A.max, A.add)
        mm("p5", 0, 128, r("Fs", 127, 128), r("SHR"), p=p1)
        ts(slot(0), r("ks"), r("p4", 0, 1), None, A.add)
        scan(row("rowB"), row("RST"), r("p5", 0, 128, p=p1), A.mult, A.max)
        mm("p5", 200, 201, row("rowB"), r("ONEF", 0, 1, p=p1))
        tc(r("nb"), slot(0))
        tt(r("nl"), slot(0), r("nb"), A.subtract)
        rows("KT", 2, 0, P, r("nb"))
        rows("KT", 3, 0, P, r("nl"))
        ts(slot(1), r("Fs"), r("p5", 200, 201), None, A.max)
        tt(slot(1), slot(1), r("KX"), A.add)
        tt(slot(2), slot(1), r("hv"), A.max)
        ts(r("off16"), slot(2), -1.0, None, A.add)
        o = ind("SW", 0, SWW, "off16", 0, 128)
        op("v", [r("VD")], [o], [lambda: V.tensor_copy(o[0], T.VD[:])])
        act(r(X, 2 * XW, 2 * XW + P), r(X, XW, XW + P), AF.Relu, -1.0)
        act(r("GK"), ind("KT", 0, P, "EL16", 0, 128), AF.Copy)
        conv("p2", 0, [("FA", "GK", 0, False, 128)])
        conv("p1", 0, [("FB", "GK", 0, False, 128)])
        conv("p0", 0, [("F1", "SW", 0, True, 128)])
        ts(r("tA"), slot(2), 2049.0, 8192.0, A.is_lt, A.mult)
        tt(r("tA"), slot(2), r("tA"), A.max)
        op("v", [r("tA")], [col(8)], [lambda: V.tensor_reduce(col(8)[0], r("tA")[0], AxisListType.X, A.min)])
        ts(col(9), col(8), -1.0, 8193.0, A.mult, A.add)
        ts(col(10), r("p7", 127, 128), -2.0, 8192.0, A.mult, A.add)
        tt(col(11), col(10), col(12), A.subtract)
        mm("p5", 0, 128, col(9), r("ID"), p=p1)
        mm("p5", 128, 256, col(11), r("ID"), p=p1)
        ts(r("ex"), r("p0", 0, 128), 0.5, None, A.is_gt)
        tt(r("eq"), r("ex"), pVF, A.mult)
        tt(r("en"), r("ex"), pQN, A.mult)
        scan(r("PF"), r("eq"), r("ZERO"), A.max, A.add)
        scan(rev("NB"), rev("en"), r("ZERO"), A.max, A.add)
        mm("p3", 0, 128, r("PF", 127, 128), r("SHR"), p=p1)
        mm("p4", 0, 128, r("NB", 0, 1), r("SHL"), p=p1)
        ts(r("nex"), r("ex"), -1.0, 1.0, A.mult, A.add)
        scan(row("rowC"), row("RST"), r("p5", 0, 128, p=p1), A.mult, A.max)
        tt(row("rowC"), row("rowC"), r("p5", 128, 256, p=p1), A.max)
        scan(row("rowA"), row("RST"), r("p3", 0, 128, p=p1), A.mult, A.max)
        mm("p3", 200, 201, row("rowA"), r("ONEF", 0, 1, p=p1))
        tt(row("rowN"), rev("rowC", p1), row("MK0"), A.mult)
        tt(row("rowT"), r("p4", 0, 128, p=p1), row("rowN"), A.max)
        scan(rev("rowD", p1), row("RST"), row("rowT"), A.mult, A.max)
        mm("p4", 200, 201, row("rowD"), r("ONEF", 0, 1, p=p1))
        tt(r("tC"), r("p2", 0, 128), r("KX"), A.subtract)
        ts(r("tD"), slot(3), -1.0, 1.0, A.mult, A.add)
        ts(slot(0), r("PF"), r("p3", 200, 201), None, A.max)
        ts(slot(1), r("p1", 0, 128), 2.0, None, A.mult)
        ts(r("NN"), r("NB"), r("p4", 200, 201), None, A.max)
        tt(slot(2), slot(0), r("NN"), A.subtract)
        tt(r("SP"), slot(0), r("NN"), A.add)
        tt(slot(2), slot(2), r("Q2"), A.is_lt)
        ts(r("s"), r("SP"), -0.5, 4095.5, A.mult, A.add)
        tt(slot(2), slot(2), r("nex"), A.add)
        tt(r("csb"), slot(2), r("s"), A.mult)
        tt(r("qq"), r("csb"), pVF, A.subtract)
        ts(r("q16"), r("qq"), -1.0, None, A.mult)
        tt(slot(1), slot(1), r("K2"), A.subtract)
        tt(slot(1), slot(1), r("tD"), A.mult)
        tt(slot(1), slot(1), r("tC"), A.add)
        tc(r("sb"), slot(1))
        tt(r("sl"), slot(1), r("sb"), A.subtract)
        rows("ST", 0, 0, P, r("sb"))
        rows("ST", 1, 0, P, r("sl"))
        ts(r("cc"), slot(2), float(XW), -1.0, A.mult, A.add)
        g2("p5", "SW", P, "q16", "F1", "GR")
        ts(r("LS16"), r("p5", 0, 128), -1.0, None, A.add)
        tt(r("L3"), r("p5", 0, 128), r("cc"), A.add)
        tc(r("L316"), r("L3"))
        g2("p2", "ST", P, "LS16", "F1", "GR")
        g2(None, X, 3 * XW, "L316", None, "XPHI")
        tt(slot(0), r("p2", 0, 128), r("V1"), A.add)
        ts(r("SBE"), slot(0), col(4), None, A.min)
        send("e", t)
        permute("v", "SBX", 0, "XPHI", (14, 15), 14)
        send("x", t)
        permute("s", XN, 0, "XPHI", range(6))
        permute("v", XN, 0, "XPHI", range(6, 14))
        ts(r(EX, 0, 128), slot(0), col(4), col(2), A.min, A.mult)
        if t == 1:
            dma("y", ext(T.y[:, 0:CUT], "y", 0, CUT), r(XN, 0, CUT))
        arrive("ae%d" % t, NE, "LE%d" % t, 0, 128)
        ts(slot(0), r("LE%d" % t), col(3), None, A.mult)
        tt(r(EX, 0, 128), slot(0), r(EX, 0, 128), A.add)
        arrive("ax%d" % t, NX, XN, CUT, P)

    def send(what, t):
        if what == "x":
            to, src, out, k, skip, rs, ls = rl[0], r("SBX"), T["RLX%d" % t][:], NX, 0, "rx%d" % t, "lx%d" % t
        else:
            to, src, out, k, skip, rs, ls = rl[1], r("SBE"), T["RLE%d" % t][:], NE, NX, "rn%d" % t, "le%d" % t
        need("g", [src], [])
        rid, pid = topo.addr(to, core)
        g.remote_dma(out, src[0], T.sem[rs], T.sem[ls], pid, rid, pick(topo, core, to, k, skip))
        count[ls] = k
        clock = dict(known["g"])
        clock[ls] = k
        note("dma", [src], [], ls, k, clock)

    def arrive(sem, k, name, lo, hi):
        count[sem] = k
        note("dma", [], [r(name, lo, hi)], sem, k, {sem: k})

    for t in range(2):
        if t:
            table_start(t)
        walks(t)
        hist()
        grow(t)
    dma("y", ext(T.ye[:], "ye"), r("E2", 0, 128))
    dma("y", ext(T.y[:, CUT:P], "y", CUT, P), r("Y2", CUT, P))
    for sem, val in count.items():
        if known["g"].get(sem, 0) < val:
            g.wait_ge(T.sem[sem], val)
